import numpy as np, ml_dtypes
CORES = [89,94,345,350]
N = 4
TK = 32
def setup_inputs(rng):
    return {"x": rng.standard_normal((N, 128, TK), dtype=np.float32).astype(ml_dtypes.bfloat16), "w1": (rng.standard_normal((N, 128, 128), dtype=np.float32) / 8).astype(ml_dtypes.bfloat16), "w2": (rng.standard_normal((N, 128, 128), dtype=np.float32) / 8).astype(ml_dtypes.bfloat16)}
def setup_inputs_big(rng):
    d = setup_inputs(rng)
    for k in ("x", "w1", "w2"): d[k] = (d[k].astype(np.float32) * 1024.0).astype(d[k].dtype)
    return d
def setup_inputs_small(rng):
    d = setup_inputs(rng)
    for k in ("x", "w1", "w2"): d[k] = (d[k].astype(np.float32) * (1 / 1024.0)).astype(d[k].dtype)
    return d
def setup_inputs_apart(rng):
    d = setup_inputs(rng)
    f = (10.0 ** rng.permutation(np.linspace(-1.5, 1.5, N))).astype(np.float32).reshape(N, 1, 1)
    for k in ("x", "w1", "w2"): d[k] = (d[k].astype(np.float32) * f).astype(d[k].dtype)
    return d
def reference(x, w1, w2):
    X, W1, W2 = x.astype(np.float64), w1.astype(np.float64), w2.astype(np.float64)
    y = np.zeros((N, 128, TK))
    for r in range(N):
        for j in range(N):
            y[r] += W2[j].T @ np.maximum(W1[j].T @ X[r], 0.0)
    return {"y": y.astype(ml_dtypes.bfloat16 if x.dtype != np.float64 else np.float64)}

@@ -1,0 +1,116 @@
+from concourse.bass import DstId, RemoteDMATransfer
+from concourse.mybir import AluOpType
+
+N = 4
+TK = 32
+D = 128
+SLOT = TK + 2 * D
+WORLD = 512
+
+SCRATCH = {
+    "pack": ("sbuf", [128, SLOT], "bfloat16"),
+    "land": ("sbuf", [128, N * SLOT], "bfloat16"),
+    "zero": ("sbuf", [128, N * TK], "float32"),
+    "h": ("sbuf", [128, N * N * TK], "bfloat16"),
+    "yo": ("sbuf", [128, N * TK], "bfloat16"),
+    "yl": ("dram", [128, TK], "bfloat16"),
+    "ph0": ("psum", [128, 512], "float32"),
+    "ph1": ("psum", [128, 512], "float32"),
+    "ph2": ("psum", [128, 512], "float32"),
+    "ph3": ("psum", [128, 512], "float32"),
+    "py": ("psum", [128, 512], "float32"),
+}
+SEMAPHORES = ["ld", "sent", "arr", "got", "st", "zs", "m2", "cp",
+              "m10", "m11", "m12", "m13", "rl0", "rl1", "rl2", "rl3"]
+
+
+def _offsets(r):
+    if r % 2 == 0:
+        return 2 * D, 0, D
+    return 0, TK, TK + D
+
+
+def _one_hop(topo, a, b):
+    if topo.same_plane(a, b):
+        return True
+    return topo.rack(topo.host(a)) != topo.rack(topo.host(b)) and topo.chip(a) == topo.chip(b)
+
+
+def _hub(T, topo):
+    for c in range(WORLD):
+        if T.rank_of(c) is None and all(
+                topo.may_write(r, c) and topo.may_write(c, r) and _one_hop(topo, r, c) for r in T.cores):
+            return c
+    return None
+
+
+def _engines(mask):
+    return [b for b in range(16) if (mask >> b) & 1]
+
+
+def _rank(g, core, T, topo, hub):
+    r = T.rank_of(core)
+    ox, o1, o2 = _offsets(r)
+    g.sync.dma_start(out=T.pack[:, o1:o1 + D], in_=T.w1[:]).then_inc(T.sem.ld, 16)
+    g.scalar.dma_start(out=T.pack[:, o2:o2 + D], in_=T.w2[:]).then_inc(T.sem.ld, 16)
+    g.sync.dma_start(out=T.pack[:, ox:ox + TK], in_=T.x[:]).then_inc(T.sem.ld, 16)
+    mask = topo.mask(core, hub)
+    ne = len(_engines(mask))
+    rid, pid = topo.addr(hub, core)
+    g.wait_ge(T.sem.ld, 48)
+    g.remote_dma(out_ap=T.land[:, r * SLOT:(r + 1) * SLOT], in_ap=T.pack[:], remote_sem=T.sem.arr, local_sem=T.sem.sent,
+                 pid=pid, routing_id=rid, dma_engine_mask=mask)
+    share = len(_engines(topo.mask(hub, core))) // N
+    g.sync.wait_ge(T.sem.got, share)
+    g.sync.dma_start(out=T.y[:], in_=T.yl[:]).then_inc(T.sem.st, 16)
+    g.sync.wait_ge(T.sem.st, 16)
+    g.wait_ge(T.sem.sent, ne)
+
+
+def _hub_program(g, core, T, topo):
+    NT = N * TK
+    ph = [T.ph0, T.ph1, T.ph2, T.ph3]
+    m1 = [T.sem.m10, T.sem.m11, T.sem.m12, T.sem.m13]
+    rl = [T.sem.rl0, T.sem.rl1, T.sem.rl2, T.sem.rl3]
+    g.vector.memset(T.zero[:], 0.0).then_inc(T.sem.zs, 1)
+    g.vector.wait_ge(T.sem.zs, 1)
+
+    g.tensor.wait_ge(T.sem.arr, sum(len(_engines(topo.mask(r, core))) for r in T.cores))
+    for j in range(N):
+        o1 = j * SLOT + _offsets(j)[1]
+        for k in range(N // 2):
+            xs = 2 * k * SLOT + _offsets(2 * k)[0]
+            g.tensor.matmul(ph[j][:, 2 * k * TK:(2 * k + 2) * TK], T.land[:, o1:o1 + D], T.land[:, xs:xs + 2 * TK],
+                            True, True).then_inc(m1[j], 1)
+    for j in range(N):
+        g.vector.wait_ge(m1[j], N // 2)
+        g.vector.tensor_tensor(T.h[:, j * NT:(j + 1) * NT], ph[j][:, 0:NT], T.zero[:], AluOpType.max).then_inc(rl[j], 1)
+    for j in range(N):
+        o2 = j * SLOT + _offsets(j)[2]
+        g.tensor.wait_ge(rl[j], 1)
+        g.tensor.matmul(T.py[:, 0:NT], T.land[:, o2:o2 + D], T.h[:, j * NT:(j + 1) * NT],
+                        j == 0, j == N - 1).then_inc(T.sem.m2, 1)
+    g.vector.wait_ge(T.sem.m2, N)
+    g.vector.tensor_copy(T.yo[:], T.py[:, 0:NT]).then_inc(T.sem.cp, 1)
+
+    trs = []
+    total = 0
+    for r, dst in enumerate(T.cores):
+        eng = _engines(topo.mask(core, dst))
+        share = len(eng) // N
+        m = sum(1 << b for b in eng[r * share:(r + 1) * share])
+        rid, pid = topo.addr(dst, core)
+        trs.append(RemoteDMATransfer(dst_ids=[DstId(rid=rid, pnc=pid)], dma_engine_mask=m, remote_sem=T.sem.got,
+                                     src=T.yo[:, r * TK:(r + 1) * TK], dst=T.yl[:]))
+        total += share
+    g.wait_ge(T.sem.cp, 1)
+    g.remote_dma_fused(trs, local_sem=T.sem.sent)
+    g.wait_ge(T.sem.sent, total)
+
+
+def rank_program(g, core, T, topo):
+    hub = _hub(T, topo)
+    if T.rank_of(core) is not None:
+        _rank(g, core, T, topo, hub)
+    elif core == hub:
+        _hub_program(g, core, T, topo)

@@ -4,104 +4,122 @@ from concourse.mybir import AluOpType
 N = 4
 TK = 32
 D = 128
-SLOT = TK + 2 * D
 WORLD = 512
 
 SCRATCH = {
-    "pack": ("sbuf", [128, SLOT], "bfloat16"),
-    "land": ("sbuf", [128, N * SLOT], "bfloat16"),
-    "zero": ("sbuf", [128, N * TK], "float32"),
-    "h": ("sbuf", [128, N * N * TK], "bfloat16"),
-    "yo": ("sbuf", [128, N * TK], "bfloat16"),
-    "yl": ("dram", [128, TK], "bfloat16"),
+    "pack": ("sbuf", [128, 2 * D + TK], "bfloat16"),
+    "wl": ("sbuf", [128, 4 * D], "bfloat16"),
+    "xl": ("sbuf", [128, 2 * TK], "bfloat16"),
+    "zero": ("sbuf", [128, 2 * TK], "float32"),
+    "h": ("sbuf", [128, 4 * TK], "bfloat16"),
+    "yo": ("sbuf", [128, 2 * TK], "bfloat16"),
+    "yl": ("sbuf", [128, TK], "bfloat16"),
     "ph0": ("psum", [128, 512], "float32"),
     "ph1": ("psum", [128, 512], "float32"),
-    "ph2": ("psum", [128, 512], "float32"),
-    "ph3": ("psum", [128, 512], "float32"),
     "py": ("psum", [128, 512], "float32"),
 }
-SEMAPHORES = ["ld", "sent", "arr", "got", "st", "zs", "m2", "cp",
-              "m10", "m11", "m12", "m13", "rl0", "rl1", "rl2", "rl3"]
-
-
-def _offsets(r):
-    if r % 2 == 0:
-        return 2 * D, 0, D
-    return 0, TK, TK + D
-
-
-def _one_hop(topo, a, b):
-    if topo.same_plane(a, b):
-        return True
-    return topo.rack(topo.host(a)) != topo.rack(topo.host(b)) and topo.chip(a) == topo.chip(b)
-
-
-def _hub(T, topo):
-    for c in range(WORLD):
-        if T.rank_of(c) is None and all(
-                topo.may_write(r, c) and topo.may_write(c, r) and _one_hop(topo, r, c) for r in T.cores):
-            return c
-    return None
+SEMAPHORES = ["ldw", "ldx", "sent", "arr", "got", "st", "zs", "m2", "cp", "m10", "m11", "rl0", "rl1"]
 
 
 def _engines(mask):
     return [b for b in range(16) if (mask >> b) & 1]
 
 
-def _rank(g, core, T, topo, hub):
-    r = T.rank_of(core)
-    ox, o1, o2 = _offsets(r)
-    g.sync.dma_start(out=T.pack[:, o1:o1 + D], in_=T.w1[:]).then_inc(T.sem.ld, 16)
-    g.scalar.dma_start(out=T.pack[:, o2:o2 + D], in_=T.w2[:]).then_inc(T.sem.ld, 16)
-    g.sync.dma_start(out=T.pack[:, ox:ox + TK], in_=T.x[:]).then_inc(T.sem.ld, 16)
-    mask = topo.mask(core, hub)
-    ne = len(_engines(mask))
-    rid, pid = topo.addr(hub, core)
-    g.wait_ge(T.sem.ld, 48)
-    g.remote_dma(out_ap=T.land[:, r * SLOT:(r + 1) * SLOT], in_ap=T.pack[:], remote_sem=T.sem.arr, local_sem=T.sem.sent,
-                 pid=pid, routing_id=rid, dma_engine_mask=mask)
-    share = len(_engines(topo.mask(hub, core))) // N
-    g.sync.wait_ge(T.sem.got, share)
-    g.sync.dma_start(out=T.y[:], in_=T.yl[:]).then_inc(T.sem.st, 16)
-    g.sync.wait_ge(T.sem.st, 16)
-    g.wait_ge(T.sem.sent, ne)
+def _bits(eng):
+    return sum(1 << b for b in eng)
 
 
-def _hub_program(g, core, T, topo):
-    NT = N * TK
-    ph = [T.ph0, T.ph1, T.ph2, T.ph3]
-    m1 = [T.sem.m10, T.sem.m11, T.sem.m12, T.sem.m13]
-    rl = [T.sem.rl0, T.sem.rl1, T.sem.rl2, T.sem.rl3]
+def _cabled(topo, a, b):
+    return topo.rack(topo.host(a)) != topo.rack(topo.host(b)) and topo.chip(a) == topo.chip(b)
+
+
+def _helper(T, topo, near, far):
+    for c in range(WORLD):
+        if T.rank_of(c) is not None:
+            continue
+        if not all(topo.may_write(r, c) and topo.may_write(c, r) for r in near + far):
+            continue
+        if all(topo.same_plane(r, c) for r in near) and all(_cabled(topo, r, c) for r in far):
+            return c
+    return None
+
+
+def _plan(T, topo):
+    hosts = sorted(set(topo.host(c) for c in T.cores))
+    groups = [[c for c in T.cores if topo.host(c) == hh] for hh in hosts]
+    return [(groups[k], _helper(T, topo, groups[k], groups[1 - k])) for k in range(2)]
+
+
+def _mlp(g, T, n, w_aps, x_ap, waits):
+    ph = [T.ph0, T.ph1]
+    m1 = [T.sem.m10, T.sem.m11]
+    rl = [T.sem.rl0, T.sem.rl1]
     g.vector.memset(T.zero[:], 0.0).then_inc(T.sem.zs, 1)
     g.vector.wait_ge(T.sem.zs, 1)
+    for k in range(2):
+        for sem, val in waits[k]:
+            g.tensor.wait_ge(sem, val)
+        g.tensor.matmul(ph[k][:, 0:n], w_aps[k][0], x_ap, True, True).then_inc(m1[k], 1)
+    for k in range(2):
+        g.vector.wait_ge(m1[k], 1)
+        g.vector.tensor_tensor(T.h[:, k * n:(k + 1) * n], ph[k][:, 0:n], T.zero[:, 0:n], AluOpType.max).then_inc(rl[k], 1)
+    for k in range(2):
+        g.tensor.wait_ge(rl[k], 1)
+        g.tensor.matmul(T.py[:, 0:n], w_aps[k][1], T.h[:, k * n:(k + 1) * n], k == 0, k == 1).then_inc(T.sem.m2, 1)
+    g.vector.wait_ge(T.sem.m2, 2)
 
-    g.tensor.wait_ge(T.sem.arr, sum(len(_engines(topo.mask(r, core))) for r in T.cores))
-    for j in range(N):
-        o1 = j * SLOT + _offsets(j)[1]
-        for k in range(N // 2):
-            xs = 2 * k * SLOT + _offsets(2 * k)[0]
-            g.tensor.matmul(ph[j][:, 2 * k * TK:(2 * k + 2) * TK], T.land[:, o1:o1 + D], T.land[:, xs:xs + 2 * TK],
-                            True, True).then_inc(m1[j], 1)
-    for j in range(N):
-        g.vector.wait_ge(m1[j], N // 2)
-        g.vector.tensor_tensor(T.h[:, j * NT:(j + 1) * NT], ph[j][:, 0:NT], T.zero[:], AluOpType.max).then_inc(rl[j], 1)
-    for j in range(N):
-        o2 = j * SLOT + _offsets(j)[2]
-        g.tensor.wait_ge(rl[j], 1)
-        g.tensor.matmul(T.py[:, 0:NT], T.land[:, o2:o2 + D], T.h[:, j * NT:(j + 1) * NT],
-                        j == 0, j == N - 1).then_inc(T.sem.m2, 1)
-    g.vector.wait_ge(T.sem.m2, N)
-    g.vector.tensor_copy(T.yo[:], T.py[:, 0:NT]).then_inc(T.sem.cp, 1)
 
+def _rank(g, core, T, topo, plan):
+    k = [i for i in range(2) if core in plan[i][0]][0]
+    mine, h_tok = plan[k]
+    h_wgt = plan[1 - k][1]
+    pos = mine.index(core)
+    mate = mine[1 - pos]
+    W = 2 * D
+    g.sync.dma_start(out=T.pack[:, 0:D], in_=T.w1[:]).then_inc(T.sem.ldw, 16)
+    g.scalar.dma_start(out=T.pack[:, D:W], in_=T.w2[:]).then_inc(T.sem.ldw, 16)
+    g.sync.dma_start(out=T.pack[:, W:W + TK], in_=T.x[:]).then_inc(T.sem.ldx, 16)
+    off = _engines(topo.mask(core, h_wgt) & topo.mask(core, h_tok))
+    e_w, e_x = off[:len(off) // 2], off[len(off) // 2:]
+    e_on = [b for b in _engines(topo.mask(core, mate)) if b not in off]
+    g.wait_ge(T.sem.ldw, 32)
+    rid, pid = topo.addr(h_wgt, core)
+    g.remote_dma(out_ap=T.wl[:, pos * W:(pos + 1) * W], in_ap=T.pack[:, 0:W], remote_sem=T.sem.arr, local_sem=T.sem.sent,
+                 pid=pid, routing_id=rid, dma_engine_mask=_bits(e_w))
+    g.wait_ge(T.sem.ldx, 16)
+    rid, pid = topo.addr(h_tok, core)
+    g.remote_dma(out_ap=T.xl[:, pos * TK:(pos + 1) * TK], in_ap=T.pack[:, W:W + TK], remote_sem=T.sem.arr,
+                 local_sem=T.sem.sent, pid=pid, routing_id=rid, dma_engine_mask=_bits(e_x))
+    rid, pid = topo.addr(mate, core)
+    g.remote_dma(out_ap=T.wl[:, 0:W], in_ap=T.pack[:, 0:W], remote_sem=T.sem.arr, local_sem=T.sem.sent,
+                 pid=pid, routing_id=rid, dma_engine_mask=_bits(e_on))
+    _mlp(g, T, TK,
+         [(T.pack[:, 0:D], T.pack[:, D:W]), (T.wl[:, 0:D], T.wl[:, D:W])], T.pack[:, W:W + TK],
+         [[(T.sem.ldw, 32), (T.sem.ldx, 16)], [(T.sem.arr, len(e_on))]])
+    g.vector.wait_ge(T.sem.got, len(_engines(topo.mask(h_tok, core))) // 2)
+    g.vector.tensor_tensor(T.yo[:, 0:TK], T.py[:, 0:TK], T.yl[:], AluOpType.add).then_inc(T.sem.cp, 1)
+    g.sync.wait_ge(T.sem.cp, 1)
+    g.sync.dma_start(out=T.y[:], in_=T.yo[:, 0:TK]).then_inc(T.sem.st, 16)
+    g.sync.wait_ge(T.sem.st, 16)
+    g.wait_ge(T.sem.sent, len(e_w) + len(e_x) + len(e_on))
+
+
+def _helper_program(g, core, T, topo, near, far):
+    W = 2 * D
+    n = 2 * TK
+    landed = sum(len(_engines(topo.mask(r, core))) // 2 for r in near + far)
+    _mlp(g, T, n,
+         [(T.wl[:, p * W:p * W + D], T.wl[:, p * W + D:(p + 1) * W]) for p in range(2)], T.xl[:],
+         [[(T.sem.arr, landed)], []])
+    g.vector.tensor_copy(T.yo[:], T.py[:, 0:n]).then_inc(T.sem.cp, 1)
     trs = []
     total = 0
-    for r, dst in enumerate(T.cores):
+    for p, dst in enumerate(near):
         eng = _engines(topo.mask(core, dst))
-        share = len(eng) // N
-        m = sum(1 << b for b in eng[r * share:(r + 1) * share])
+        share = len(eng) // 2
         rid, pid = topo.addr(dst, core)
-        trs.append(RemoteDMATransfer(dst_ids=[DstId(rid=rid, pnc=pid)], dma_engine_mask=m, remote_sem=T.sem.got,
-                                     src=T.yo[:, r * TK:(r + 1) * TK], dst=T.yl[:]))
+        trs.append(RemoteDMATransfer(dst_ids=[DstId(rid=rid, pnc=pid)], dma_engine_mask=_bits(eng[p * share:(p + 1) * share]),
+                                     remote_sem=T.sem.got, src=T.yo[:, p * TK:(p + 1) * TK], dst=T.yl[:]))
         total += share
     g.wait_ge(T.sem.cp, 1)
     g.remote_dma_fused(trs, local_sem=T.sem.sent)
@@ -109,8 +127,10 @@ def _hub_program(g, core, T, topo):
 
 
 def rank_program(g, core, T, topo):
-    hub = _hub(T, topo)
+    plan = _plan(T, topo)
     if T.rank_of(core) is not None:
-        _rank(g, core, T, topo, hub)
-    elif core == hub:
-        _hub_program(g, core, T, topo)
+        _rank(g, core, T, topo, plan)
+        return
+    for k in range(2):
+        if core == plan[k][1]:
+            _helper_program(g, core, T, topo, plan[k][0], plan[1 - k][0])

@@ -39,7 +39,7 @@ def _helper(T, topo, near, far):
             continue
         if not all(topo.may_write(r, c) and topo.may_write(c, r) for r in near + far):
             continue
-        if all(topo.same_plane(r, c) for r in near) and all(_cabled(topo, r, c) for r in far):
+        if all(_cabled(topo, r, c) for r in near) and all(topo.same_plane(r, c) for r in far):
             return c
     return None
 
@@ -80,7 +80,7 @@ def _rank(g, core, T, topo, plan):
     g.scalar.dma_start(out=T.pack[:, D:W], in_=T.w2[:]).then_inc(T.sem.ldw, 16)
     g.sync.dma_start(out=T.pack[:, W:W + TK], in_=T.x[:]).then_inc(T.sem.ldx, 16)
     off = _engines(topo.mask(core, h_wgt) & topo.mask(core, h_tok))
-    e_w, e_x = off[:len(off) // 2], off[len(off) // 2:]
+    e_w, e_x = off[0::2], off[1::2]
     e_on = [b for b in _engines(topo.mask(core, mate)) if b not in off]
     g.wait_ge(T.sem.ldw, 32)
     rid, pid = topo.addr(h_wgt, core)

from concourse.bass import DstId, RemoteDMATransfer
from concourse.mybir import AluOpType

N = 4
TK = 32
D = 128
WORLD = 512

SCRATCH = {
    "pack": ("sbuf", [128, 2 * D + TK], "bfloat16"),
    "wl": ("sbuf", [128, 4 * D], "bfloat16"),
    "xl": ("sbuf", [128, 2 * TK], "bfloat16"),
    "zero": ("sbuf", [128, 2 * TK], "float32"),
    "h": ("sbuf", [128, 4 * TK], "bfloat16"),
    "yo": ("sbuf", [128, 2 * TK], "bfloat16"),
    "yl": ("sbuf", [128, TK], "bfloat16"),
    "ph0": ("psum", [128, 512], "float32"),
    "ph1": ("psum", [128, 512], "float32"),
    "py": ("psum", [128, 512], "float32"),
}
SEMAPHORES = ["ldw", "ldx", "sent", "arr", "got", "st", "zs", "m2", "cp", "m10", "m11", "rl0", "rl1"]


def _engines(mask):
    return [b for b in range(16) if (mask >> b) & 1]


def _bits(eng):
    return sum(1 << b for b in eng)


def _cabled(topo, a, b):
    return topo.rack(topo.host(a)) != topo.rack(topo.host(b)) and topo.chip(a) == topo.chip(b)


def _helper(T, topo, near, far):
    for c in range(WORLD):
        if T.rank_of(c) is not None:
            continue
        if not all(topo.may_write(r, c) and topo.may_write(c, r) for r in near + far):
            continue
        if all(_cabled(topo, r, c) for r in near) and all(topo.same_plane(r, c) for r in far):
            return c
    return None


def _plan(T, topo):
    hosts = sorted(set(topo.host(c) for c in T.cores))
    groups = [[c for c in T.cores if topo.host(c) == hh] for hh in hosts]
    return [(groups[k], _helper(T, topo, groups[k], groups[1 - k])) for k in range(2)]


def _mlp(g, T, n, w_aps, x_ap, waits):
    ph = [T.ph0, T.ph1]
    m1 = [T.sem.m10, T.sem.m11]
    rl = [T.sem.rl0, T.sem.rl1]
    g.vector.memset(T.zero[:], 0.0).then_inc(T.sem.zs, 1)
    g.vector.wait_ge(T.sem.zs, 1)
    for k in range(2):
        for sem, val in waits[k]:
            g.tensor.wait_ge(sem, val)
        g.tensor.matmul(ph[k][:, 0:n], w_aps[k][0], x_ap, True, True).then_inc(m1[k], 1)
    for k in range(2):
        g.vector.wait_ge(m1[k], 1)
        g.vector.tensor_tensor(T.h[:, k * n:(k + 1) * n], ph[k][:, 0:n], T.zero[:, 0:n], AluOpType.max).then_inc(rl[k], 1)
    for k in range(2):
        g.tensor.wait_ge(rl[k], 1)
        g.tensor.matmul(T.py[:, 0:n], w_aps[k][1], T.h[:, k * n:(k + 1) * n], k == 0, k == 1).then_inc(T.sem.m2, 1)
    g.vector.wait_ge(T.sem.m2, 2)


def _rank(g, core, T, topo, plan):
    k = [i for i in range(2) if core in plan[i][0]][0]
    mine, h_tok = plan[k]
    h_wgt = plan[1 - k][1]
    pos = mine.index(core)
    mate = mine[1 - pos]
    W = 2 * D
    g.sync.dma_start(out=T.pack[:, 0:D], in_=T.w1[:]).then_inc(T.sem.ldw, 16)
    g.scalar.dma_start(out=T.pack[:, D:W], in_=T.w2[:]).then_inc(T.sem.ldw, 16)
    g.sync.dma_start(out=T.pack[:, W:W + TK], in_=T.x[:]).then_inc(T.sem.ldx, 16)
    off = _engines(topo.mask(core, h_wgt) & topo.mask(core, h_tok))
    e_w, e_x = off[0::2], off[1::2]
    e_on = [b for b in _engines(topo.mask(core, mate)) if b not in off]
    g.wait_ge(T.sem.ldw, 32)
    rid, pid = topo.addr(h_wgt, core)
    g.remote_dma(out_ap=T.wl[:, pos * W:(pos + 1) * W], in_ap=T.pack[:, 0:W], remote_sem=T.sem.arr, local_sem=T.sem.sent,
                 pid=pid, routing_id=rid, dma_engine_mask=_bits(e_w))
    g.wait_ge(T.sem.ldx, 16)
    rid, pid = topo.addr(h_tok, core)
    g.remote_dma(out_ap=T.xl[:, pos * TK:(pos + 1) * TK], in_ap=T.pack[:, W:W + TK], remote_sem=T.sem.arr,
                 local_sem=T.sem.sent, pid=pid, routing_id=rid, dma_engine_mask=_bits(e_x))
    rid, pid = topo.addr(mate, core)
    g.remote_dma(out_ap=T.wl[:, 0:W], in_ap=T.pack[:, 0:W], remote_sem=T.sem.arr, local_sem=T.sem.sent,
                 pid=pid, routing_id=rid, dma_engine_mask=_bits(e_on))
    _mlp(g, T, TK,
         [(T.pack[:, 0:D], T.pack[:, D:W]), (T.wl[:, 0:D], T.wl[:, D:W])], T.pack[:, W:W + TK],
         [[(T.sem.ldw, 32), (T.sem.ldx, 16)], [(T.sem.arr, len(e_on))]])
    g.vector.wait_ge(T.sem.got, len(_engines(topo.mask(h_tok, core))) // 2)
    g.vector.tensor_tensor(T.yo[:, 0:TK], T.py[:, 0:TK], T.yl[:], AluOpType.add).then_inc(T.sem.cp, 1)
    g.sync.wait_ge(T.sem.cp, 1)
    g.sync.dma_start(out=T.y[:], in_=T.yo[:, 0:TK]).then_inc(T.sem.st, 16)
    g.sync.wait_ge(T.sem.st, 16)
    g.wait_ge(T.sem.sent, len(e_w) + len(e_x) + len(e_on))


def _helper_program(g, core, T, topo, near, far):
    W = 2 * D
    n = 2 * TK
    landed = sum(len(_engines(topo.mask(r, core))) // 2 for r in near + far)
    _mlp(g, T, n,
         [(T.wl[:, p * W:p * W + D], T.wl[:, p * W + D:(p + 1) * W]) for p in range(2)], T.xl[:],
         [[(T.sem.arr, landed)], []])
    g.vector.tensor_copy(T.yo[:], T.py[:, 0:n]).then_inc(T.sem.cp, 1)
    trs = []
    total = 0
    for p, dst in enumerate(near):
        eng = _engines(topo.mask(core, dst))
        share = len(eng) // 2
        rid, pid = topo.addr(dst, core)
        trs.append(RemoteDMATransfer(dst_ids=[DstId(rid=rid, pnc=pid)], dma_engine_mask=_bits(eng[p * share:(p + 1) * share]),
                                     remote_sem=T.sem.got, src=T.yo[:, p * TK:(p + 1) * TK], dst=T.yl[:]))
        total += share
    g.wait_ge(T.sem.cp, 1)
    g.remote_dma_fused(trs, local_sem=T.sem.sent)
    g.wait_ge(T.sem.sent, total)


def rank_program(g, core, T, topo):
    plan = _plan(T, topo)
    if T.rank_of(core) is not None:
        _rank(g, core, T, topo, plan)
        return
    for k in range(2):
        if core == plan[k][1]:
            _helper_program(g, core, T, topo, plan[k][0], plan[1 - k][0])
